import numpy as np
import ml_dtypes


def mxq(x, axis, fmt="e4m3"):
    dtype, down = {"e4m3": (ml_dtypes.float8_e4m3fn, 7), "e5m2": (ml_dtypes.float8_e5m2, 14)}[fmt]
    v = np.moveaxis(np.asarray(x, np.float32).astype(ml_dtypes.bfloat16).astype(np.float64), axis, -1)
    blocks = v.reshape(v.shape[:-1] + (-1, 32))
    amax = np.abs(blocks).max(-1, keepdims=True)
    byte = np.maximum(np.where(amax > 0, np.frexp(amax)[1] - 1 + 127, 0) - down, 1)
    scale = np.exp2(byte - 127.0)
    codes = (blocks / scale).astype(np.float32).astype(dtype).astype(np.float64)
    return np.moveaxis((codes * scale).reshape(v.shape), -1, axis)


WIDE = False


def mx_kscale(k):
    if not WIDE:
        return np.ones(k)
    levels = np.array([10, -10, 5, -5, 0])
    if k % 512:
        return np.exp2(np.random.permutation(np.resize(levels, k // 32))).repeat(32)
    a = np.empty((k // 512, 16))
    for p in range(k // 512):
        a[p, :8] = np.random.permutation(np.resize(levels, 8))
        for g in range(8):
            far = levels[np.abs(levels - a[p, g]) >= 10]
            a[p, g + 8] = far[np.random.randint(len(far))]
    return np.exp2(a.ravel()).repeat(32)


def f64(x):
    return np.asarray(x).astype(np.float64)


def striped(idx):
    return np.tile(idx.reshape(-1, 16).T, (8, 1)).astype(np.uint16)


def unstriped(offs):
    return offs[:16].T.reshape(-1).astype(np.int64)


def striped8(idx):
    return np.concatenate([x.reshape(-1, 16).T for x in idx]).astype(np.uint16)


def runs(offs, k):
    lists = np.stack([offs[16 * r : 16 * r + 16].T.reshape(-1) for r in range(8)]).astype(np.int64)
    return lists[np.arange(k) % 512 // 64]


def pack_weight(w):
    k, n = w.shape
    w = f64(np.asarray(w, np.float32).astype(ml_dtypes.bfloat16)).reshape(k // 32, 32, n)
    amax = np.abs(w).max(1)
    byte = np.clip(np.where(amax > 0, np.frexp(amax)[1] - 1 + 127 - 7, 1), 1, 254)
    scaled = (w * np.exp2(127.0 - byte)[:, None, :]).reshape(k, n).astype(np.float32)
    words = np.ascontiguousarray(scaled.reshape(k // 512, 128, 4, n).transpose(0, 1, 3, 2)).astype(ml_dtypes.float8_e4m3fn).view(np.uint8)
    return words, np.ascontiguousarray(byte.astype(np.uint8).reshape(k // 512, 16, n))


def unpack_weight(words, scales):
    g, p, n, _ = words.shape
    vals = np.ascontiguousarray(words).view(ml_dtypes.float8_e4m3fn).astype(np.float64) * np.repeat(np.exp2(scales.astype(np.float64) - 127.0), 8, axis=1)[..., None]
    return vals.transpose(0, 1, 3, 2).reshape(g * 512, n)


def sigmoid(v):
    return 1.0 / (1.0 + np.exp(-np.maximum(v, -700.0)))


K, T, S, H, G = 512, 2048, 512, 512, 2048


def setup_inputs():
    n = np.random.standard_normal
    s = mx_kscale(K)[:, None]
    packed_xT = pack_weight(n((K, T)) * s)
    packed_dT = pack_weight(n((K, G)) / s)
    return {
        "x_words": packed_xT[0],
        "x_scales": packed_xT[1],
        "w1": (n((K, H)) / np.sqrt(K) / s).astype(np.float32),
        "gs": (np.random.uniform(0.5, 1.5, (K, 1)) * s).astype(np.float32),
        "d_words": packed_dT[0],
        "d_scales": packed_dT[1],
        "offs": striped(np.random.permutation(T)[:S]),
        "n1": striped8(np.stack([np.random.permutation(S) for _ in range(8)])),
        "n2": striped8(np.stack([np.random.permutation(S) for _ in range(8)])),
        "n3": striped8(np.stack([np.random.permutation(S) for _ in range(8)])),
        "k1": striped8(np.random.randint(0, G, (8, H))),
        "n4": striped8(np.stack([np.random.permutation(S) for _ in range(8)])),
        "n5": striped8(np.stack([np.random.permutation(S) for _ in range(8)])),
    }


def reference(x_words, x_scales, w1, gs, d_words, d_scales, offs, n1, n2, n3, k1, n4, n5):
    d_k1 = unpack_weight(d_words, d_scales)[np.arange(K)[:, None], runs(k1, K)]
    xq = unpack_weight(x_words, x_scales)[:, unstriped(offs)]
    y = mxq(f64(w1), 0, "e4m3").T @ xq
    z = f64(gs) * (y + y[np.arange(H)[:, None], runs(n1, H)] - (np.maximum(y[np.arange(H)[:, None], runs(n2, H)], y[np.arange(H)[:, None], runs(n3, H)])))
    h = 0.0625 * ((d_k1.T @ mxq(z, 0, "e4m3")))
    st = h * (sigmoid(h[np.arange(H)[:, None], runs(n4, H)]))
    return st - (st[np.arange(H)[:, None], runs(n5, H)])

@@ -1,0 +1,204 @@
+from contextlib import ExitStack
+
+import concourse.mybir as mybir
+
+F32 = mybir.dt.float32
+BF16 = mybir.dt.bfloat16
+I32 = mybir.dt.int32
+U32 = mybir.dt.uint32
+U16 = mybir.dt.uint16
+U8 = mybir.dt.uint8
+FP8X4 = mybir.dt.float8_e4m3fn_x4
+ALU = mybir.AluOpType
+ACT = mybir.ActivationFunctionType
+
+P = 128
+PACK = 4
+S = 512
+TABLE = 2048
+WIN = 1024
+HALF = 256
+FLOPS = 2 * 2 * 512 * 512 * 512
+
+
+def tile_picked_densetrimhopg_none_p_kernel(
+    tc, x_words, x_scales, w1, gs, d_words, d_scales, offs, n1, n2, n3, k1, n4, n5, out
+):
+    nc = tc.nc
+    with ExitStack() as ctx:
+        lists = ctx.enter_context(tc.tile_pool(name="lists", bufs=1))
+        keep = ctx.enter_context(tc.tile_pool(name="keep", bufs=1))
+        psum = ctx.enter_context(tc.psum_pool(name="psum", bufs=1))
+
+        def load_list(name, src):
+            tile = lists.tile([P, S // 16], U16, name=name)
+            nc.sync.dma_start(tile[:], src)
+            return tile
+
+        def words_of(packed):
+            return packed[0].rearrange("p n t -> p (n t)").bitcast(I32)
+
+        xs_win = keep.tile([P, TABLE], U8, name="xs_win", align_bytes=64)
+        nc.gpsimd.memset(xs_win[:].bitcast(I32), 0)
+        ds_win = keep.tile([P, TABLE], U8, name="ds_win", align_bytes=64)
+        nc.gpsimd.memset(ds_win[:].bitcast(I32), 0)
+        ds_plane = keep.tile([P, S], U8, name="ds_plane", align_bytes=64)
+        nc.gpsimd.memset(ds_plane[:].bitcast(I32), 0)
+
+        offs_t = load_list("offs_t", offs)
+        w_raw = keep.tile([P, PACK, S], F32, name="w_raw", align_bytes=64)
+        nc.sync.dma_start(w_raw[:], w1.rearrange("(p j) c -> p j c", j=PACK))
+        xs_rows = x_scales[0].bitcast(I32)
+        for r in range(PACK):
+            nc.sync.dma_start(xs_win[:].bitcast(I32)[r:P:32, :], xs_rows[r:16:4, :])
+        xw_win = keep.tile([P, TABLE], I32, name="xw_win", align_bytes=64)
+        nc.sync.dma_start(xw_win[:], words_of(x_words))
+        k1_t = load_list("k1_t", k1)
+        ds_rows = d_scales[0].bitcast(I32)
+        for r in range(2):
+            nc.sync.dma_start(ds_win[:].bitcast(I32)[r:P:16, :], ds_rows[r:16:2, :])
+        n2_t = load_list("n2_t", n2)
+        n3_t = load_list("n3_t", n3)
+        n1_t = load_list("n1_t", n1)
+        gs_t = keep.tile([P, PACK], F32, name="gs_t")
+        nc.sync.dma_start(gs_t[:], gs.rearrange("(p t) o -> p (t o)", t=PACK))
+        dw_win = keep.tile([P, TABLE], I32, name="dw_win", align_bytes=64)
+        nc.sync.dma_start(dw_win[:], words_of(d_words))
+        n4_t = load_list("n4_t", n4)
+        n5_t = load_list("n5_t", n5)
+
+        w_codes = keep.tile([P, S], U32, name="w_codes", align_bytes=64)
+        w_scales = keep.tile([P, S], U8, name="w_scales", align_bytes=64)
+        w_bf = []
+        for h in range(2):
+            grouped = keep.tile([P, PACK * HALF], BF16, name="w_bf%d" % h, align_bytes=64)
+            dst = grouped[:].rearrange("p (t m j) -> p m t j", t=PACK, j=PACK)
+            srcv = w_raw[:, :, h * HALF : (h + 1) * HALF].rearrange("p j (m t) -> p m t j", t=PACK)
+            if h == 0:
+                nc.vector.tensor_copy(dst, srcv)
+            else:
+                nc.scalar.copy(dst, srcv)
+            w_bf.append(grouped)
+        xs_g = keep.tile([P, S], U8, name="xs_g", align_bytes=64)
+        nc.vector.tensor_copy(xs_g[:], xs_win[:].indirect(offs_t[:]))
+        for h in range(2):
+            for t in range(PACK):
+                cols = slice(P * t + 64 * h, P * t + 64 * (h + 1))
+                nc.vector.quantize_mx(
+                    out=w_codes[:, cols].bitcast(FP8X4),
+                    scales=w_scales[:, cols],
+                    in_=w_bf[h][:, HALF * t : HALF * (t + 1)],
+                )
+        xw_g = keep.tile([P, S], U32, name="xw_g", align_bytes=64)
+        nc.vector.tensor_copy(xw_g[:], xw_win[:].bitcast(U32).indirect(offs_t[:]))
+        y_ps = []
+        for t in range(PACK):
+            acc = psum.tile([P, S], F32, name="y_ps%d" % t)
+            cols = slice(P * t, P * (t + 1))
+            nc.tensor.matmul_mx(
+                out=acc[:],
+                lhsT=w_codes[:, cols].bitcast(FP8X4),
+                lhsT_scale=w_scales[:, cols],
+                rhs=xw_g[:].bitcast(FP8X4),
+                rhs_scale=xs_g[:],
+                start=True,
+                stop=True,
+            )
+            y_ps.append(acc)
+
+        ds_g = keep.tile([P, S], U8, name="ds_g", align_bytes=64)
+        nc.vector.tensor_copy(ds_g[:], ds_win[:].indirect(k1_t[:]))
+        ds_dealt = keep.tile([P, S], U8, name="ds_dealt", align_bytes=64)
+        nc.vector.tensor_copy(
+            ds_dealt[:].rearrange("p (t m) -> p t m", t=PACK), ds_g[:].rearrange("p (m t) -> p t m", t=PACK)
+        )
+        for r in range(PACK):
+            first = 16 * (r // 2) + r % 2
+            nc.sync.dma_start(ds_plane[:].bitcast(I32)[r:P:32, :], ds_dealt[:].bitcast(I32)[first:P:32, :])
+
+        win = [keep.tile([P, WIN], F32, name="win%d" % t) for t in range(PACK)]
+        plain = [keep.tile([P, S], F32, name="plain%d" % t) for t in range(PACK)]
+        for t in range(PACK):
+            nc.scalar.copy(win[t][:, 0:S], y_ps[t][:])
+            nc.scalar.copy(plain[t][:], y_ps[t][:])
+
+        da = [keep.tile([P, S], F32, name="da%d" % t) for t in range(PACK)]
+        db = [keep.tile([P, S], F32, name="db%d" % t) for t in range(PACK)]
+        dmax = [keep.tile([P, S], F32, name="dmax%d" % t) for t in range(PACK)]
+        zs = [keep.tile([P, S], F32, name="zs%d" % t) for t in range(PACK)]
+        z_bf = keep.tile([P, S, PACK], BF16, name="z_bf", align_bytes=64)
+
+        def step_a(t):
+            nc.vector.tensor_tensor(da[t][:], win[t][:].indirect(n2_t[:]), plain[t][:], ALU.subtract)
+
+        def step_b(t):
+            nc.vector.tensor_tensor(db[t][:], win[t][:].indirect(n3_t[:]), plain[t][:], ALU.subtract)
+
+        def step_m(t):
+            nc.vector.tensor_tensor(dmax[t][:], da[t][:], db[t][:], ALU.max)
+
+        def step_s(t):
+            nc.vector.tensor_tensor(zs[t][:], win[t][:].indirect(n1_t[:]), dmax[t][:], ALU.subtract)
+            nc.scalar.activation(z_bf[:, :, t], zs[t][:], ACT.Copy, scale=gs_t[:, t : t + 1])
+
+        dw_g = keep.tile([P, S], U32, name="dw_g", align_bytes=64)
+        dw_dealt = keep.tile([P, S], U32, name="dw_dealt", align_bytes=64)
+        for t in (0, 2):
+            step_a(t)
+            if t > 0:
+                step_s(t - 1)
+            step_b(t)
+            step_a(t + 1)
+            step_m(t)
+            step_b(t + 1)
+            step_s(t)
+            step_m(t + 1)
+        nc.vector.tensor_copy(dw_g[:], dw_win[:].bitcast(U32).indirect(k1_t[:]))
+        step_s(3)
+        nc.vector.tensor_copy(
+            dw_dealt[:].rearrange("p (t m) -> p m t", t=PACK), dw_g[:].rearrange("p (m t) -> p m t", t=PACK)
+        )
+
+        z_codes = keep.tile([P, S], U32, name="z_codes", align_bytes=64)
+        z_scales = keep.tile([P, S], U8, name="z_scales", align_bytes=64)
+        nc.vector.quantize_mx(
+            out=z_codes[:].bitcast(FP8X4), scales=z_scales[:], in_=z_bf[:].rearrange("p j t -> p (j t)")
+        )
+
+        hwin = [keep.tile([P, WIN], F32, name="hwin%d" % t) for t in range(PACK)]
+        swin = [keep.tile([P, WIN], F32, name="swin%d" % t) for t in range(PACK)]
+        gate = [keep.tile([P, S], F32, name="gate%d" % t) for t in range(PACK)]
+        st = [keep.tile([P, S], F32, name="st%d" % t) for t in range(PACK)]
+        res = [keep.tile([P, S], F32, name="res%d" % t) for t in range(PACK)]
+        out_rows = out.rearrange("(p t) j -> t p j", t=PACK)
+        for t in range(PACK):
+            acc = psum.tile([P, S], F32, name="h_ps%d" % t)
+            cols = slice(P * t, P * (t + 1))
+            nc.tensor.matmul_mx(
+                out=acc[:],
+                lhsT=dw_dealt[:, cols].bitcast(FP8X4),
+                lhsT_scale=ds_plane[:, cols],
+                rhs=z_codes[:].bitcast(FP8X4),
+                rhs_scale=z_scales[:],
+                start=True,
+                stop=True,
+            )
+            if t in (1, 2):
+                nc.vector.tensor_scalar(hwin[t][:, 0:S], acc[:], 0.0625, None, ALU.mult)
+            else:
+                nc.scalar.activation(hwin[t][:, 0:S], acc[:], ACT.Copy, scale=0.0625)
+            nc.scalar.activation(gate[t][:], hwin[t][:].indirect(n4_t[:]), ACT.Sigmoid)
+
+        def finish(t):
+            nc.vector.tensor_tensor(res[t][:], swin[t][:].indirect(n5_t[:]), st[t][:], ALU.add)
+            nc.sync.dma_start(out_rows[t], res[t][:])
+
+        for t in range(PACK):
+            nc.vector.tensor_tensor(st[t][:], gate[t][:], hwin[t][:, 0:S], ALU.mult)
+            if t > 0:
+                finish(t - 1)
+            if t < 2:
+                nc.vector.tensor_scalar(swin[t][:, 0:S], st[t][:], -1.0, None, ALU.mult)
+            else:
+                nc.scalar.activation(swin[t][:, 0:S], st[t][:], ACT.Copy, scale=-1.0)
+        finish(PACK - 1)

@@ -19,6 +19,8 @@ TABLE = 2048
 WIN = 1024
 HALF = 256
 FLOPS = 2 * 2 * 512 * 512 * 512
+HALVES = (slice(0, HALF), slice(HALF, S))
+LIST_HALVES = (slice(0, HALF // 16), slice(HALF // 16, S // 16))
 
 
 def tile_picked_densetrimhopg_none_p_kernel(
@@ -38,25 +40,40 @@ def tile_picked_densetrimhopg_none_p_kernel(
         def words_of(packed):
             return packed[0].rearrange("p n t -> p (n t)").bitcast(I32)
 
+        def product(acc, codes, scales, t, moving, moving_scales):
+            cols = slice(P * t, P * (t + 1))
+            nc.tensor.matmul_mx(
+                out=acc,
+                lhsT=codes[:, cols].bitcast(FP8X4),
+                lhsT_scale=scales[:, cols],
+                rhs=moving.bitcast(FP8X4),
+                rhs_scale=moving_scales,
+                start=True,
+                stop=True,
+            )
+
+        ds_win = keep.tile([P, TABLE], U8, name="ds_win", tag="after_ds", align_bytes=64)
+        nc.gpsimd.memset(ds_win[:].bitcast(I32), 0)
         xs_win = keep.tile([P, TABLE], U8, name="xs_win", align_bytes=64)
         nc.gpsimd.memset(xs_win[:].bitcast(I32), 0)
-        ds_win = keep.tile([P, TABLE], U8, name="ds_win", align_bytes=64)
-        nc.gpsimd.memset(ds_win[:].bitcast(I32), 0)
+        warm = keep.tile([P, 2], F32, name="warm")
+        nc.gpsimd.memset(warm[:, 0:1], 0.0)
         ds_plane = keep.tile([P, S], U8, name="ds_plane", align_bytes=64)
         nc.gpsimd.memset(ds_plane[:].bitcast(I32), 0)
 
         offs_t = load_list("offs_t", offs)
+        xs_rows = x_scales[0].bitcast(I32)
+        xs_in = keep.tile([P, TABLE // 4], I32, name="xs_in", align_bytes=64)
+        for r in range(PACK):
+            queue = nc.sync if r < 2 else nc.scalar
+            queue.dma_start(xs_in[r:P:32, :], xs_rows[r:16:4, :])
         w_raw = keep.tile([P, PACK, S], F32, name="w_raw", align_bytes=64)
         nc.sync.dma_start(w_raw[:], w1.rearrange("(p j) c -> p j c", j=PACK))
-        xs_rows = x_scales[0].bitcast(I32)
-        for r in range(PACK):
-            nc.sync.dma_start(xs_win[:].bitcast(I32)[r:P:32, :], xs_rows[r:16:4, :])
-        xw_win = keep.tile([P, TABLE], I32, name="xw_win", align_bytes=64)
-        nc.sync.dma_start(xw_win[:], words_of(x_words))
         k1_t = load_list("k1_t", k1)
-        ds_rows = d_scales[0].bitcast(I32)
-        for r in range(2):
-            nc.sync.dma_start(ds_win[:].bitcast(I32)[r:P:16, :], ds_rows[r:16:2, :])
+        nc.scalar.dma_start(ds_win[:].bitcast(I32)[0:P:8, :], d_scales[0].bitcast(I32))
+        nc.scalar.activation(warm[:, 1:2], warm[:, 0:1], ACT.Sigmoid)
+        xw_win = keep.tile([P, TABLE], I32, name="xw_win", tag="after_xw", align_bytes=64)
+        nc.sync.dma_start(xw_win[:], words_of(x_words))
         n2_t = load_list("n2_t", n2)
         n3_t = load_list("n3_t", n3)
         n1_t = load_list("n1_t", n1)
@@ -67,69 +84,63 @@ def tile_picked_densetrimhopg_none_p_kernel(
         n4_t = load_list("n4_t", n4)
         n5_t = load_list("n5_t", n5)
 
-        w_codes = keep.tile([P, S], U32, name="w_codes", align_bytes=64)
-        w_scales = keep.tile([P, S], U8, name="w_scales", align_bytes=64)
-        w_bf = []
-        for h in range(2):
-            grouped = keep.tile([P, PACK * HALF], BF16, name="w_bf%d" % h, align_bytes=64)
-            dst = grouped[:].rearrange("p (t m j) -> p m t j", t=PACK, j=PACK)
-            srcv = w_raw[:, :, h * HALF : (h + 1) * HALF].rearrange("p j (m t) -> p m t j", t=PACK)
-            if h == 0:
-                nc.vector.tensor_copy(dst, srcv)
-            else:
-                nc.scalar.copy(dst, srcv)
-            w_bf.append(grouped)
+        for q in range(PACK):
+            rows = slice(32 * q, 32 * q + 4)
+            nc.vector.tensor_copy(xs_win[:].bitcast(I32)[rows, :], xs_in[rows, :])
         xs_g = keep.tile([P, S], U8, name="xs_g", align_bytes=64)
         nc.vector.tensor_copy(xs_g[:], xs_win[:].indirect(offs_t[:]))
-        for h in range(2):
-            for t in range(PACK):
-                cols = slice(P * t + 64 * h, P * t + 64 * (h + 1))
-                nc.vector.quantize_mx(
-                    out=w_codes[:, cols].bitcast(FP8X4),
-                    scales=w_scales[:, cols],
-                    in_=w_bf[h][:, HALF * t : HALF * (t + 1)],
-                )
-        xw_g = keep.tile([P, S], U32, name="xw_g", align_bytes=64)
-        nc.vector.tensor_copy(xw_g[:], xw_win[:].bitcast(U32).indirect(offs_t[:]))
-        y_ps = []
-        for t in range(PACK):
-            acc = psum.tile([P, S], F32, name="y_ps%d" % t)
-            cols = slice(P * t, P * (t + 1))
-            nc.tensor.matmul_mx(
-                out=acc[:],
-                lhsT=w_codes[:, cols].bitcast(FP8X4),
-                lhsT_scale=w_scales[:, cols],
-                rhs=xw_g[:].bitcast(FP8X4),
-                rhs_scale=xs_g[:],
-                start=True,
-                stop=True,
-            )
-            y_ps.append(acc)
 
-        ds_g = keep.tile([P, S], U8, name="ds_g", align_bytes=64)
+        w_view = w_raw[:].rearrange("p j (m t) -> p m t j", t=PACK)
+        w_lo = keep.tile([P, 2 * S], BF16, name="w_lo", align_bytes=64)
+        w_hi = keep.tile([P, 2 * S], BF16, name="w_hi", align_bytes=64)
+        nc.scalar.copy(w_lo[:].rearrange("p (t m j) -> p m t j", t=2, j=PACK), w_view[:, :, 0:2, :])
+        nc.scalar.copy(w_hi[:].rearrange("p (t m j) -> p m t j", t=2, j=PACK), w_view[:, :, 2:4, :])
+
+        ds_g = keep.tile([P, S], U8, name="ds_g", tag="after_deal", align_bytes=64)
         nc.vector.tensor_copy(ds_g[:], ds_win[:].indirect(k1_t[:]))
-        ds_dealt = keep.tile([P, S], U8, name="ds_dealt", align_bytes=64)
+
+        def quantize_w(grouped, name, tag):
+            codes = keep.tile([P, HALF], U32, name=name + "_codes", align_bytes=64)
+            scales = keep.tile([P, HALF], U8, name=name + "_scales", tag=tag, align_bytes=64)
+            nc.vector.quantize_mx(out=codes[:].bitcast(FP8X4), scales=scales[:], in_=grouped[:])
+            return codes, scales
+
+        lo_codes, lo_scales = quantize_w(w_lo, "lo", "lo_scales")
+
+        xw_g = keep.tile([P, S], U32, name="xw_g", tag="after_ds", align_bytes=64)
+        win = [keep.tile([P, WIN], F32, name="win%d" % t) for t in range(PACK)]
+        plain = [keep.tile([P, S], F32, name="plain%d" % t) for t in range(PACK)]
+        for u in range(2):
+            nc.vector.tensor_copy(xw_g[:, HALVES[u]], xw_win[:].bitcast(U32).indirect(offs_t[:, LIST_HALVES[u]]))
+            acc = psum.tile([P, HALF], F32, name="y_half%d" % u, tag="half%d" % u)
+            product(acc[:], lo_codes, lo_scales, 0, xw_g[:, HALVES[u]], xs_g[:, HALVES[u]])
+            nc.scalar.copy(win[0][:, HALVES[u]], acc[:])
+            nc.scalar.copy(plain[0][:, HALVES[u]], acc[:])
+        ds_dealt = keep.tile([P, S], U8, name="ds_dealt", tag="after_xw", align_bytes=64)
         nc.vector.tensor_copy(
             ds_dealt[:].rearrange("p (t m) -> p t m", t=PACK), ds_g[:].rearrange("p (m t) -> p t m", t=PACK)
         )
         for r in range(PACK):
-            first = 16 * (r // 2) + r % 2
-            nc.sync.dma_start(ds_plane[:].bitcast(I32)[r:P:32, :], ds_dealt[:].bitcast(I32)[first:P:32, :])
-
-        win = [keep.tile([P, WIN], F32, name="win%d" % t) for t in range(PACK)]
-        plain = [keep.tile([P, S], F32, name="plain%d" % t) for t in range(PACK)]
-        for t in range(PACK):
-            nc.scalar.copy(win[t][:, 0:S], y_ps[t][:])
-            nc.scalar.copy(plain[t][:], y_ps[t][:])
+            nc.sync.dma_start(ds_plane[:].bitcast(I32)[r:P:32, :], ds_dealt[:].bitcast(I32)[8 * r : P : 32, :])
+        hi_codes, hi_scales = quantize_w(w_hi, "hi", "after_deal")
+        for t in range(1, PACK):
+            acc = psum.tile([P, S], F32, name="y_ps%d" % t, tag="bank%d" % t)
+            codes, scales = (lo_codes, lo_scales) if t < 2 else (hi_codes, hi_scales)
+            product(acc[:], codes, scales, t % 2, xw_g[:], xs_g[:])
+            nc.scalar.copy(win[t][:, 0:S], acc[:])
+            nc.scalar.copy(plain[t][:], acc[:])
 
         da = [keep.tile([P, S], F32, name="da%d" % t) for t in range(PACK)]
         db = [keep.tile([P, S], F32, name="db%d" % t) for t in range(PACK)]
-        dmax = [keep.tile([P, S], F32, name="dmax%d" % t) for t in range(PACK)]
+        dmax = [keep.tile([P, S], F32, name="dmax%d" % t, tag="dmax%d" % t, align_bytes=64) for t in range(PACK)]
         zs = [keep.tile([P, S], F32, name="zs%d" % t) for t in range(PACK)]
         z_bf = keep.tile([P, S, PACK], BF16, name="z_bf", align_bytes=64)
+        whole = (slice(0, S), slice(0, S // 16))
+        parts = list(zip(HALVES, LIST_HALVES))
 
-        def step_a(t):
-            nc.vector.tensor_tensor(da[t][:], win[t][:].indirect(n2_t[:]), plain[t][:], ALU.subtract)
+        def step_a(t, part=whole):
+            cols, entries = part
+            nc.vector.tensor_tensor(da[t][:, cols], win[t][:].indirect(n2_t[:, entries]), plain[t][:, cols], ALU.subtract)
 
         def step_b(t):
             nc.vector.tensor_tensor(db[t][:], win[t][:].indirect(n3_t[:]), plain[t][:], ALU.subtract)
@@ -137,33 +148,49 @@ def tile_picked_densetrimhopg_none_p_kernel(
         def step_m(t):
             nc.vector.tensor_tensor(dmax[t][:], da[t][:], db[t][:], ALU.max)
 
-        def step_s(t):
-            nc.vector.tensor_tensor(zs[t][:], win[t][:].indirect(n1_t[:]), dmax[t][:], ALU.subtract)
-            nc.scalar.activation(z_bf[:, :, t], zs[t][:], ACT.Copy, scale=gs_t[:, t : t + 1])
+        def step_s(t, part=whole):
+            cols, entries = part
+            nc.vector.tensor_tensor(zs[t][:, cols], win[t][:].indirect(n1_t[:, entries]), dmax[t][:, cols], ALU.subtract)
+            nc.scalar.activation(z_bf[:, cols, t], zs[t][:, cols], ACT.Copy, scale=gs_t[:, t : t + 1])
 
-        dw_g = keep.tile([P, S], U32, name="dw_g", align_bytes=64)
+        step_a(0, parts[0])
+        step_a(0, parts[1])
+        step_b(0)
+        step_a(1)
+        step_m(0)
+        step_b(1)
+        step_s(0)
+        step_m(1)
+        step_a(2)
+        step_s(1)
+        step_b(2)
+        step_a(3)
+        step_m(2)
+        step_b(3)
+        step_s(2, parts[0])
+        step_m(3)
+        step_s(2, parts[1])
+        step_s(3, parts[0])
+        step_s(3, parts[1])
+
+        dw_g = keep.tile([P, S], U32, name="dw_g", tag="dmax3", align_bytes=64)
         dw_dealt = keep.tile([P, S], U32, name="dw_dealt", align_bytes=64)
-        for t in (0, 2):
-            step_a(t)
-            if t > 0:
-                step_s(t - 1)
-            step_b(t)
-            step_a(t + 1)
-            step_m(t)
-            step_b(t + 1)
-            step_s(t)
-            step_m(t + 1)
         nc.vector.tensor_copy(dw_g[:], dw_win[:].bitcast(U32).indirect(k1_t[:]))
-        step_s(3)
+        z_codes = keep.tile([P, S], U32, name="z_codes", align_bytes=64)
+        z_scales = keep.tile([P, S], U8, name="z_scales", align_bytes=64)
+
+        def quantize_z(cols):
+            nc.vector.quantize_mx(
+                out=z_codes[:, cols].bitcast(FP8X4),
+                scales=z_scales[:, cols],
+                in_=z_bf[:, cols, :].rearrange("p j t -> p (j t)"),
+            )
+
+        quantize_z(HALVES[0])
         nc.vector.tensor_copy(
             dw_dealt[:].rearrange("p (t m) -> p m t", t=PACK), dw_g[:].rearrange("p (m t) -> p m t", t=PACK)
         )
-
-        z_codes = keep.tile([P, S], U32, name="z_codes", align_bytes=64)
-        z_scales = keep.tile([P, S], U8, name="z_scales", align_bytes=64)
-        nc.vector.quantize_mx(
-            out=z_codes[:].bitcast(FP8X4), scales=z_scales[:], in_=z_bf[:].rearrange("p j t -> p (j t)")
-        )
+        quantize_z(HALVES[1])
 
         hwin = [keep.tile([P, WIN], F32, name="hwin%d" % t) for t in range(PACK)]
         swin = [keep.tile([P, WIN], F32, name="swin%d" % t) for t in range(PACK)]
@@ -171,34 +198,46 @@ def tile_picked_densetrimhopg_none_p_kernel(
         st = [keep.tile([P, S], F32, name="st%d" % t) for t in range(PACK)]
         res = [keep.tile([P, S], F32, name="res%d" % t) for t in range(PACK)]
         out_rows = out.rearrange("(p t) j -> t p j", t=PACK)
-        for t in range(PACK):
-            acc = psum.tile([P, S], F32, name="h_ps%d" % t)
-            cols = slice(P * t, P * (t + 1))
-            nc.tensor.matmul_mx(
-                out=acc[:],
-                lhsT=dw_dealt[:, cols].bitcast(FP8X4),
-                lhsT_scale=ds_plane[:, cols],
-                rhs=z_codes[:].bitcast(FP8X4),
-                rhs_scale=z_scales[:],
-                start=True,
-                stop=True,
-            )
-            if t in (1, 2):
-                nc.vector.tensor_scalar(hwin[t][:, 0:S], acc[:], 0.0625, None, ALU.mult)
-            else:
-                nc.scalar.activation(hwin[t][:, 0:S], acc[:], ACT.Copy, scale=0.0625)
+        for u in range(2):
+            acc = psum.tile([P, HALF], F32, name="h_half%d" % u, tag="half%d" % u)
+            product(acc[:], dw_dealt, ds_plane, 0, z_codes[:, HALVES[u]], z_scales[:, HALVES[u]])
+            nc.scalar.activation(hwin[0][:, HALVES[u]], acc[:], ACT.Copy, scale=0.0625)
+        h_ps = {}
+        for t in range(1, PACK):
+            h_ps[t] = psum.tile([P, S], F32, name="h_ps%d" % t, tag="bank%d" % t)
+            product(h_ps[t][:], dw_dealt, ds_plane, t, z_codes[:], z_scales[:])
+
+        def gate_of(t):
             nc.scalar.activation(gate[t][:], hwin[t][:].indirect(n4_t[:]), ACT.Sigmoid)
 
-        def finish(t):
-            nc.vector.tensor_tensor(res[t][:], swin[t][:].indirect(n5_t[:]), st[t][:], ALU.add)
-            nc.sync.dma_start(out_rows[t], res[t][:])
-
-        for t in range(PACK):
+        def gated(t):
             nc.vector.tensor_tensor(st[t][:], gate[t][:], hwin[t][:, 0:S], ALU.mult)
-            if t > 0:
-                finish(t - 1)
-            if t < 2:
-                nc.vector.tensor_scalar(swin[t][:, 0:S], st[t][:], -1.0, None, ALU.mult)
-            else:
-                nc.scalar.activation(swin[t][:, 0:S], st[t][:], ACT.Copy, scale=-1.0)
-        finish(PACK - 1)
+
+        def negate(t):
+            nc.scalar.activation(swin[t][:, 0:S], st[t][:], ACT.Copy, scale=-1.0)
+
+        def finish(t, part=whole):
+            cols, entries = part
+            nc.vector.tensor_tensor(res[t][:, cols], swin[t][:].indirect(n5_t[:, entries]), st[t][:, cols], ALU.add)
+            nc.sync.dma_start(out_rows[t][:, cols], res[t][:, cols])
+
+        gate_of(0)
+        for t in (1, 2):
+            nc.vector.tensor_scalar(hwin[t][:, 0:S], h_ps[t][:], 0.0625, None, ALU.mult)
+        gate_of(1)
+        nc.scalar.activation(hwin[3][:, 0:S], h_ps[3][:], ACT.Copy, scale=0.0625)
+        gate_of(2)
+        gated(0)
+        nc.vector.tensor_scalar(swin[0][:, 0:S], st[0][:], -1.0, None, ALU.mult)
+        gated(1)
+        negate(1)
+        gate_of(3)
+        finish(0)
+        gated(2)
+        negate(2)
+        finish(1)
+        gated(3)
+        negate(3)
+        finish(2)
+        finish(3, parts[0])
+        finish(3, parts[1])

@@ -40,12 +40,14 @@ def tile_picked_densetrimhopg_none_p_kernel(
         def words_of(packed):
             return packed[0].rearrange("p n t -> p (n t)").bitcast(I32)
 
-        def product(acc, codes, scales, t, moving, moving_scales):
-            cols = slice(P * t, P * (t + 1))
+        def block(tile, t):
+            return tile[:, P * t : P * (t + 1)]
+
+        def product(acc, codes, scales, moving, moving_scales):
             nc.tensor.matmul_mx(
                 out=acc,
-                lhsT=codes[:, cols].bitcast(FP8X4),
-                lhsT_scale=scales[:, cols],
+                lhsT=codes.bitcast(FP8X4),
+                lhsT_scale=scales,
                 rhs=moving.bitcast(FP8X4),
                 rhs_scale=moving_scales,
                 start=True,
@@ -113,7 +115,7 @@ def tile_picked_densetrimhopg_none_p_kernel(
         for u in range(2):
             nc.vector.tensor_copy(xw_g[:, HALVES[u]], xw_win[:].bitcast(U32).indirect(offs_t[:, LIST_HALVES[u]]))
             acc = psum.tile([P, HALF], F32, name="y_half%d" % u, tag="half%d" % u)
-            product(acc[:], lo_codes, lo_scales, 0, xw_g[:, HALVES[u]], xs_g[:, HALVES[u]])
+            product(acc[:], block(lo_codes, 0), block(lo_scales, 0), xw_g[:, HALVES[u]], xs_g[:, HALVES[u]])
             nc.scalar.copy(win[0][:, HALVES[u]], acc[:])
             nc.scalar.copy(plain[0][:, HALVES[u]], acc[:])
         ds_dealt = keep.tile([P, S], U8, name="ds_dealt", tag="after_xw", align_bytes=64)
@@ -126,7 +128,7 @@ def tile_picked_densetrimhopg_none_p_kernel(
         for t in range(1, PACK):
             acc = psum.tile([P, S], F32, name="y_ps%d" % t, tag="bank%d" % t)
             codes, scales = (lo_codes, lo_scales) if t < 2 else (hi_codes, hi_scales)
-            product(acc[:], codes, scales, t % 2, xw_g[:], xs_g[:])
+            product(acc[:], block(codes, t % 2), block(scales, t % 2), xw_g[:], xs_g[:])
             nc.scalar.copy(win[t][:, 0:S], acc[:])
             nc.scalar.copy(plain[t][:], acc[:])
 
@@ -174,7 +176,7 @@ def tile_picked_densetrimhopg_none_p_kernel(
         step_s(3, parts[1])
 
         dw_g = keep.tile([P, S], U32, name="dw_g", tag="dmax3", align_bytes=64)
-        dw_dealt = keep.tile([P, S], U32, name="dw_dealt", align_bytes=64)
+        dw_dealt = [keep.tile([P, HALF], U32, name="dw_dealt%d" % u, align_bytes=64) for u in range(2)]
         nc.vector.tensor_copy(dw_g[:], dw_win[:].bitcast(U32).indirect(k1_t[:]))
         z_codes = keep.tile([P, S], U32, name="z_codes", align_bytes=64)
         z_scales = keep.tile([P, S], U8, name="z_scales", align_bytes=64)
@@ -186,26 +188,32 @@ def tile_picked_densetrimhopg_none_p_kernel(
                 in_=z_bf[:, cols, :].rearrange("p j t -> p (j t)"),
             )
 
-        quantize_z(HALVES[0])
-        nc.vector.tensor_copy(
-            dw_dealt[:].rearrange("p (t m) -> p m t", t=PACK), dw_g[:].rearrange("p (m t) -> p m t", t=PACK)
-        )
-        quantize_z(HALVES[1])
+        dw_cols = dw_g[:].rearrange("p (m t) -> p m t", t=PACK)
+        for u in range(2):
+            quantize_z(HALVES[u])
+            nc.vector.tensor_copy(
+                dw_dealt[u][:].rearrange("p (t m) -> p m t", t=2), dw_cols[:, :, 2 * u : 2 * u + 2]
+            )
 
         hwin = [keep.tile([P, WIN], F32, name="hwin%d" % t) for t in range(PACK)]
         swin = [keep.tile([P, WIN], F32, name="swin%d" % t) for t in range(PACK)]
-        gate = [keep.tile([P, S], F32, name="gate%d" % t) for t in range(PACK)]
+        gate = {t: keep.tile([P, S], F32, name="gate%d" % t) for t in range(1, PACK)}
         st = [keep.tile([P, S], F32, name="st%d" % t) for t in range(PACK)]
         res = [keep.tile([P, S], F32, name="res%d" % t) for t in range(PACK)]
         out_rows = out.rearrange("(p t) j -> t p j", t=PACK)
+        h_plain = keep.tile([P, S], F32, name="h_plain")
         for u in range(2):
-            acc = psum.tile([P, HALF], F32, name="h_half%d" % u, tag="half%d" % u)
-            product(acc[:], dw_dealt, ds_plane, 0, z_codes[:, HALVES[u]], z_scales[:, HALVES[u]])
-            nc.scalar.activation(hwin[0][:, HALVES[u]], acc[:], ACT.Copy, scale=0.0625)
+            first = psum.tile([P, HALF], F32, name="h0_half%d" % u, tag="half%d" % u)
+            product(first[:], block(dw_dealt[0], 0), block(ds_plane, 0), z_codes[:, HALVES[u]], z_scales[:, HALVES[u]])
+            second = psum.tile([P, HALF], F32, name="h1_half%d" % u, tag="bank%d" % u)
+            product(second[:], block(dw_dealt[0], 1), block(ds_plane, 1), z_codes[:, HALVES[u]], z_scales[:, HALVES[u]])
+            nc.scalar.activation(hwin[0][:, HALVES[u]], first[:], ACT.Sigmoid, scale=0.0625)
+            nc.scalar.activation(h_plain[:, HALVES[u]], first[:], ACT.Copy, scale=0.0625)
+            nc.vector.tensor_scalar(hwin[1][:, HALVES[u]], second[:], 0.0625, None, ALU.mult)
         h_ps = {}
-        for t in range(1, PACK):
+        for t in range(2, PACK):
             h_ps[t] = psum.tile([P, S], F32, name="h_ps%d" % t, tag="bank%d" % t)
-            product(h_ps[t][:], dw_dealt, ds_plane, t, z_codes[:], z_scales[:])
+            product(h_ps[t][:], block(dw_dealt[1], t - 2), block(ds_plane, t), z_codes[:], z_scales[:])
 
         def gate_of(t):
             nc.scalar.activation(gate[t][:], hwin[t][:].indirect(n4_t[:]), ACT.Sigmoid)
@@ -221,21 +229,22 @@ def tile_picked_densetrimhopg_none_p_kernel(
             nc.vector.tensor_tensor(res[t][:, cols], swin[t][:].indirect(n5_t[:, entries]), st[t][:, cols], ALU.add)
             nc.sync.dma_start(out_rows[t][:, cols], res[t][:, cols])
 
-        gate_of(0)
-        for t in (1, 2):
-            nc.vector.tensor_scalar(hwin[t][:, 0:S], h_ps[t][:], 0.0625, None, ALU.mult)
+        def scale_out(t):
+            nc.scalar.activation(hwin[t][:, 0:S], h_ps[t][:], ACT.Copy, scale=0.0625)
+
+        nc.vector.tensor_tensor(st[0][:], hwin[0][:].indirect(n4_t[:]), h_plain[:], ALU.mult)
         gate_of(1)
-        nc.scalar.activation(hwin[3][:, 0:S], h_ps[3][:], ACT.Copy, scale=0.0625)
+        scale_out(2)
+        scale_out(3)
         gate_of(2)
-        gated(0)
         nc.vector.tensor_scalar(swin[0][:, 0:S], st[0][:], -1.0, None, ALU.mult)
         gated(1)
         negate(1)
         gate_of(3)
         finish(0)
         gated(2)
-        negate(2)
         finish(1)
+        nc.vector.tensor_scalar(swin[2][:, 0:S], st[2][:], -1.0, None, ALU.mult)
         gated(3)
         negate(3)
         finish(2)

@@ -98,7 +98,7 @@ def tile_picked_densetrimhopg_none_p_kernel(
         nc.scalar.copy(w_lo[:].rearrange("p (t m j) -> p m t j", t=2, j=PACK), w_view[:, :, 0:2, :])
         nc.scalar.copy(w_hi[:].rearrange("p (t m j) -> p m t j", t=2, j=PACK), w_view[:, :, 2:4, :])
 
-        ds_g = keep.tile([P, S], U8, name="ds_g", tag="after_deal", align_bytes=64)
+        ds_g = keep.tile([P, S], U8, name="ds_g", align_bytes=64)
         nc.vector.tensor_copy(ds_g[:], ds_win[:].indirect(k1_t[:]))
 
         def quantize_w(grouped, name, tag):
@@ -108,6 +108,12 @@ def tile_picked_densetrimhopg_none_p_kernel(
             return codes, scales
 
         lo_codes, lo_scales = quantize_w(w_lo, "lo", "lo_scales")
+        ds_dealt = keep.tile([P, S], U8, name="ds_dealt", align_bytes=64)
+        nc.vector.tensor_copy(
+            ds_dealt[:].rearrange("p (t m) -> p t m", t=PACK), ds_g[:].rearrange("p (m t) -> p t m", t=PACK)
+        )
+        for r in range(PACK):
+            nc.sync.dma_start(ds_plane[:].bitcast(I32)[r:P:32, :], ds_dealt[:].bitcast(I32)[8 * r : P : 32, :])
 
         xw_g = keep.tile([P, S], U32, name="xw_g", tag="after_ds", align_bytes=64)
         win = [keep.tile([P, WIN], F32, name="win%d" % t) for t in range(PACK)]
@@ -118,13 +124,7 @@ def tile_picked_densetrimhopg_none_p_kernel(
             product(acc[:], block(lo_codes, 0), block(lo_scales, 0), xw_g[:, HALVES[u]], xs_g[:, HALVES[u]])
             nc.scalar.copy(win[0][:, HALVES[u]], acc[:])
             nc.scalar.copy(plain[0][:, HALVES[u]], acc[:])
-        ds_dealt = keep.tile([P, S], U8, name="ds_dealt", tag="after_xw", align_bytes=64)
-        nc.vector.tensor_copy(
-            ds_dealt[:].rearrange("p (t m) -> p t m", t=PACK), ds_g[:].rearrange("p (m t) -> p t m", t=PACK)
-        )
-        for r in range(PACK):
-            nc.sync.dma_start(ds_plane[:].bitcast(I32)[r:P:32, :], ds_dealt[:].bitcast(I32)[8 * r : P : 32, :])
-        hi_codes, hi_scales = quantize_w(w_hi, "hi", "after_deal")
+        hi_codes, hi_scales = quantize_w(w_hi, "hi", "after_xw")
         for t in range(1, PACK):
             acc = psum.tile([P, S], F32, name="y_ps%d" % t, tag="bank%d" % t)
             codes, scales = (lo_codes, lo_scales) if t < 2 else (hi_codes, hi_scales)
@@ -175,7 +175,7 @@ def tile_picked_densetrimhopg_none_p_kernel(
         step_s(3, parts[0])
         step_s(3, parts[1])
 
-        dw_g = keep.tile([P, S], U32, name="dw_g", tag="dmax3", align_bytes=64)
+        dw_g = keep.tile([P, S], U32, name="dw_g", tag="dmax2", align_bytes=64)
         dw_dealt = [keep.tile([P, HALF], U32, name="dw_dealt%d" % u, align_bytes=64) for u in range(2)]
         nc.vector.tensor_copy(dw_g[:], dw_win[:].bitcast(U32).indirect(k1_t[:]))
         z_codes = keep.tile([P, S], U32, name="z_codes", align_bytes=64)
@@ -243,8 +243,8 @@ def tile_picked_densetrimhopg_none_p_kernel(
         gate_of(3)
         finish(0)
         gated(2)
+        negate(2)
         finish(1)
-        nc.vector.tensor_scalar(swin[2][:, 0:S], st[2][:], -1.0, None, ALU.mult)
         gated(3)
         negate(3)
         finish(2)

from contextlib import ExitStack

import concourse.mybir as mybir

F32 = mybir.dt.float32
BF16 = mybir.dt.bfloat16
I32 = mybir.dt.int32
U32 = mybir.dt.uint32
U16 = mybir.dt.uint16
U8 = mybir.dt.uint8
FP8X4 = mybir.dt.float8_e4m3fn_x4
ALU = mybir.AluOpType
ACT = mybir.ActivationFunctionType

P = 128
PACK = 4
S = 512
TABLE = 2048
WIN = 1024
HALF = 256
FLOPS = 2 * 2 * 512 * 512 * 512
HALVES = (slice(0, HALF), slice(HALF, S))
LIST_HALVES = (slice(0, HALF // 16), slice(HALF // 16, S // 16))


def tile_picked_densetrimhopg_none_p_kernel(
    tc, x_words, x_scales, w1, gs, d_words, d_scales, offs, n1, n2, n3, k1, n4, n5, out
):
    nc = tc.nc
    with ExitStack() as ctx:
        lists = ctx.enter_context(tc.tile_pool(name="lists", bufs=1))
        keep = ctx.enter_context(tc.tile_pool(name="keep", bufs=1))
        psum = ctx.enter_context(tc.psum_pool(name="psum", bufs=1))

        def load_list(name, src):
            tile = lists.tile([P, S // 16], U16, name=name)
            nc.sync.dma_start(tile[:], src)
            return tile

        def words_of(packed):
            return packed[0].rearrange("p n t -> p (n t)").bitcast(I32)

        def block(tile, t):
            return tile[:, P * t : P * (t + 1)]

        def product(acc, codes, scales, moving, moving_scales):
            nc.tensor.matmul_mx(
                out=acc,
                lhsT=codes.bitcast(FP8X4),
                lhsT_scale=scales,
                rhs=moving.bitcast(FP8X4),
                rhs_scale=moving_scales,
                start=True,
                stop=True,
            )

        ds_win = keep.tile([P, TABLE], U8, name="ds_win", tag="after_ds", align_bytes=64)
        nc.gpsimd.memset(ds_win[:].bitcast(I32), 0)
        xs_win = keep.tile([P, TABLE], U8, name="xs_win", align_bytes=64)
        nc.gpsimd.memset(xs_win[:].bitcast(I32), 0)
        warm = keep.tile([P, 2], F32, name="warm")
        nc.gpsimd.memset(warm[:, 0:1], 0.0)
        ds_plane = keep.tile([P, S], U8, name="ds_plane", align_bytes=64)
        nc.gpsimd.memset(ds_plane[:].bitcast(I32), 0)

        offs_t = load_list("offs_t", offs)
        xs_rows = x_scales[0].bitcast(I32)
        xs_in = keep.tile([P, TABLE // 4], I32, name="xs_in", align_bytes=64)
        for r in range(PACK):
            queue = nc.sync if r < 2 else nc.scalar
            queue.dma_start(xs_in[r:P:32, :], xs_rows[r:16:4, :])
        w_raw = keep.tile([P, PACK, S], F32, name="w_raw", align_bytes=64)
        nc.sync.dma_start(w_raw[:], w1.rearrange("(p j) c -> p j c", j=PACK))
        k1_t = load_list("k1_t", k1)
        nc.scalar.dma_start(ds_win[:].bitcast(I32)[0:P:8, :], d_scales[0].bitcast(I32))
        nc.scalar.activation(warm[:, 1:2], warm[:, 0:1], ACT.Sigmoid)
        xw_win = keep.tile([P, TABLE], I32, name="xw_win", tag="after_xw", align_bytes=64)
        nc.sync.dma_start(xw_win[:], words_of(x_words))
        n2_t = load_list("n2_t", n2)
        n3_t = load_list("n3_t", n3)
        n1_t = load_list("n1_t", n1)
        gs_t = keep.tile([P, PACK], F32, name="gs_t")
        nc.sync.dma_start(gs_t[:], gs.rearrange("(p t) o -> p (t o)", t=PACK))
        dw_win = keep.tile([P, TABLE], I32, name="dw_win", align_bytes=64)
        nc.sync.dma_start(dw_win[:], words_of(d_words))
        n4_t = load_list("n4_t", n4)
        n5_t = load_list("n5_t", n5)

        for q in range(PACK):
            rows = slice(32 * q, 32 * q + 4)
            nc.vector.tensor_copy(xs_win[:].bitcast(I32)[rows, :], xs_in[rows, :])
        xs_g = keep.tile([P, S], U8, name="xs_g", align_bytes=64)
        nc.vector.tensor_copy(xs_g[:], xs_win[:].indirect(offs_t[:]))

        w_view = w_raw[:].rearrange("p j (m t) -> p m t j", t=PACK)
        w_lo = keep.tile([P, 2 * S], BF16, name="w_lo", align_bytes=64)
        w_hi = keep.tile([P, 2 * S], BF16, name="w_hi", align_bytes=64)
        nc.scalar.copy(w_lo[:].rearrange("p (t m j) -> p m t j", t=2, j=PACK), w_view[:, :, 0:2, :])
        nc.scalar.copy(w_hi[:].rearrange("p (t m j) -> p m t j", t=2, j=PACK), w_view[:, :, 2:4, :])

        ds_g = keep.tile([P, S], U8, name="ds_g", align_bytes=64)
        nc.vector.tensor_copy(ds_g[:], ds_win[:].indirect(k1_t[:]))

        def quantize_w(grouped, name, tag):
            codes = keep.tile([P, HALF], U32, name=name + "_codes", align_bytes=64)
            scales = keep.tile([P, HALF], U8, name=name + "_scales", tag=tag, align_bytes=64)
            nc.vector.quantize_mx(out=codes[:].bitcast(FP8X4), scales=scales[:], in_=grouped[:])
            return codes, scales

        lo_codes, lo_scales = quantize_w(w_lo, "lo", "lo_scales")
        ds_dealt = keep.tile([P, S], U8, name="ds_dealt", align_bytes=64)
        nc.vector.tensor_copy(
            ds_dealt[:].rearrange("p (t m) -> p t m", t=PACK), ds_g[:].rearrange("p (m t) -> p t m", t=PACK)
        )
        for r in range(PACK):
            nc.sync.dma_start(ds_plane[:].bitcast(I32)[r:P:32, :], ds_dealt[:].bitcast(I32)[8 * r : P : 32, :])

        xw_g = keep.tile([P, S], U32, name="xw_g", tag="after_ds", align_bytes=64)
        win = [keep.tile([P, WIN], F32, name="win%d" % t) for t in range(PACK)]
        plain = [keep.tile([P, S], F32, name="plain%d" % t) for t in range(PACK)]
        for u in range(2):
            nc.vector.tensor_copy(xw_g[:, HALVES[u]], xw_win[:].bitcast(U32).indirect(offs_t[:, LIST_HALVES[u]]))
            acc = psum.tile([P, HALF], F32, name="y_half%d" % u, tag="half%d" % u)
            product(acc[:], block(lo_codes, 0), block(lo_scales, 0), xw_g[:, HALVES[u]], xs_g[:, HALVES[u]])
            nc.scalar.copy(win[0][:, HALVES[u]], acc[:])
            nc.scalar.copy(plain[0][:, HALVES[u]], acc[:])
        hi_codes, hi_scales = quantize_w(w_hi, "hi", "after_xw")
        for t in range(1, PACK):
            acc = psum.tile([P, S], F32, name="y_ps%d" % t, tag="bank%d" % t)
            codes, scales = (lo_codes, lo_scales) if t < 2 else (hi_codes, hi_scales)
            product(acc[:], block(codes, t % 2), block(scales, t % 2), xw_g[:], xs_g[:])
            nc.scalar.copy(win[t][:, 0:S], acc[:])
            nc.scalar.copy(plain[t][:], acc[:])

        da = [keep.tile([P, S], F32, name="da%d" % t) for t in range(PACK)]
        db = [keep.tile([P, S], F32, name="db%d" % t) for t in range(PACK)]
        dmax = [keep.tile([P, S], F32, name="dmax%d" % t, tag="dmax%d" % t, align_bytes=64) for t in range(PACK)]
        zs = [keep.tile([P, S], F32, name="zs%d" % t) for t in range(PACK)]
        z_bf = keep.tile([P, S, PACK], BF16, name="z_bf", align_bytes=64)
        whole = (slice(0, S), slice(0, S // 16))
        parts = list(zip(HALVES, LIST_HALVES))

        def step_a(t, part=whole):
            cols, entries = part
            nc.vector.tensor_tensor(da[t][:, cols], win[t][:].indirect(n2_t[:, entries]), plain[t][:, cols], ALU.subtract)

        def step_b(t):
            nc.vector.tensor_tensor(db[t][:], win[t][:].indirect(n3_t[:]), plain[t][:], ALU.subtract)

        def step_m(t):
            nc.vector.tensor_tensor(dmax[t][:], da[t][:], db[t][:], ALU.max)

        def step_s(t, part=whole):
            cols, entries = part
            nc.vector.tensor_tensor(zs[t][:, cols], win[t][:].indirect(n1_t[:, entries]), dmax[t][:, cols], ALU.subtract)
            nc.scalar.activation(z_bf[:, cols, t], zs[t][:, cols], ACT.Copy, scale=gs_t[:, t : t + 1])

        step_a(0, parts[0])
        step_a(0, parts[1])
        step_b(0)
        step_a(1)
        step_m(0)
        step_b(1)
        step_s(0)
        step_m(1)
        step_a(2)
        step_s(1)
        step_b(2)
        step_a(3)
        step_m(2)
        step_b(3)
        step_s(2, parts[0])
        step_m(3)
        step_s(2, parts[1])
        step_s(3, parts[0])
        step_s(3, parts[1])

        dw_g = keep.tile([P, S], U32, name="dw_g", tag="dmax2", align_bytes=64)
        dw_dealt = [keep.tile([P, HALF], U32, name="dw_dealt%d" % u, align_bytes=64) for u in range(2)]
        nc.vector.tensor_copy(dw_g[:], dw_win[:].bitcast(U32).indirect(k1_t[:]))
        z_codes = keep.tile([P, S], U32, name="z_codes", align_bytes=64)
        z_scales = keep.tile([P, S], U8, name="z_scales", align_bytes=64)

        def quantize_z(cols):
            nc.vector.quantize_mx(
                out=z_codes[:, cols].bitcast(FP8X4),
                scales=z_scales[:, cols],
                in_=z_bf[:, cols, :].rearrange("p j t -> p (j t)"),
            )

        dw_cols = dw_g[:].rearrange("p (m t) -> p m t", t=PACK)
        for u in range(2):
            quantize_z(HALVES[u])
            nc.vector.tensor_copy(
                dw_dealt[u][:].rearrange("p (t m) -> p m t", t=2), dw_cols[:, :, 2 * u : 2 * u + 2]
            )

        hwin = [keep.tile([P, WIN], F32, name="hwin%d" % t) for t in range(PACK)]
        swin = [keep.tile([P, WIN], F32, name="swin%d" % t) for t in range(PACK)]
        gate = {t: keep.tile([P, S], F32, name="gate%d" % t) for t in range(1, PACK)}
        st = [keep.tile([P, S], F32, name="st%d" % t) for t in range(PACK)]
        res = [keep.tile([P, S], F32, name="res%d" % t) for t in range(PACK)]
        out_rows = out.rearrange("(p t) j -> t p j", t=PACK)
        h_plain = keep.tile([P, S], F32, name="h_plain")
        for u in range(2):
            first = psum.tile([P, HALF], F32, name="h0_half%d" % u, tag="half%d" % u)
            product(first[:], block(dw_dealt[0], 0), block(ds_plane, 0), z_codes[:, HALVES[u]], z_scales[:, HALVES[u]])
            second = psum.tile([P, HALF], F32, name="h1_half%d" % u, tag="bank%d" % u)
            product(second[:], block(dw_dealt[0], 1), block(ds_plane, 1), z_codes[:, HALVES[u]], z_scales[:, HALVES[u]])
            nc.scalar.activation(hwin[0][:, HALVES[u]], first[:], ACT.Sigmoid, scale=0.0625)
            nc.scalar.activation(h_plain[:, HALVES[u]], first[:], ACT.Copy, scale=0.0625)
            nc.vector.tensor_scalar(hwin[1][:, HALVES[u]], second[:], 0.0625, None, ALU.mult)
        h_ps = {}
        for t in range(2, PACK):
            h_ps[t] = psum.tile([P, S], F32, name="h_ps%d" % t, tag="bank%d" % t)
            product(h_ps[t][:], block(dw_dealt[1], t - 2), block(ds_plane, t), z_codes[:], z_scales[:])

        def gate_of(t):
            nc.scalar.activation(gate[t][:], hwin[t][:].indirect(n4_t[:]), ACT.Sigmoid)

        def gated(t):
            nc.vector.tensor_tensor(st[t][:], gate[t][:], hwin[t][:, 0:S], ALU.mult)

        def negate(t):
            nc.scalar.activation(swin[t][:, 0:S], st[t][:], ACT.Copy, scale=-1.0)

        def finish(t, part=whole):
            cols, entries = part
            nc.vector.tensor_tensor(res[t][:, cols], swin[t][:].indirect(n5_t[:, entries]), st[t][:, cols], ALU.add)
            nc.sync.dma_start(out_rows[t][:, cols], res[t][:, cols])

        def scale_out(t):
            nc.scalar.activation(hwin[t][:, 0:S], h_ps[t][:], ACT.Copy, scale=0.0625)

        nc.vector.tensor_tensor(st[0][:], hwin[0][:].indirect(n4_t[:]), h_plain[:], ALU.mult)
        gate_of(1)
        scale_out(2)
        scale_out(3)
        gate_of(2)
        nc.vector.tensor_scalar(swin[0][:, 0:S], st[0][:], -1.0, None, ALU.mult)
        gated(1)
        negate(1)
        gate_of(3)
        finish(0)
        gated(2)
        negate(2)
        finish(1)
        gated(3)
        negate(3)
        finish(2)
        finish(3, parts[0])
        finish(3, parts[1])
